import numpy as np
import ml_dtypes


def mxq(x, axis, fmt="e4m3"):
    dtype, down = {"e4m3": (ml_dtypes.float8_e4m3fn, 7), "e5m2": (ml_dtypes.float8_e5m2, 14)}[fmt]
    v = np.moveaxis(np.asarray(x, np.float32).astype(ml_dtypes.bfloat16).astype(np.float64), axis, -1)
    blocks = v.reshape(v.shape[:-1] + (-1, 32))
    amax = np.abs(blocks).max(-1, keepdims=True)
    byte = np.maximum(np.where(amax > 0, np.frexp(amax)[1] - 1 + 127, 0) - down, 1)
    scale = np.exp2(byte - 127.0)
    codes = (blocks / scale).astype(np.float32).astype(dtype).astype(np.float64)
    return np.moveaxis((codes * scale).reshape(v.shape), -1, axis)


WIDE = False


def mx_kscale(k):
    if not WIDE:
        return np.ones(k)
    levels = np.array([10, -10, 5, -5, 0])
    if k % 512:
        return np.exp2(np.random.permutation(np.resize(levels, k // 32))).repeat(32)
    a = np.empty((k // 512, 16))
    for p in range(k // 512):
        a[p, :8] = np.random.permutation(np.resize(levels, 8))
        for g in range(8):
            far = levels[np.abs(levels - a[p, g]) >= 10]
            a[p, g + 8] = far[np.random.randint(len(far))]
    return np.exp2(a.ravel()).repeat(32)


def f64(x):
    return np.asarray(x).astype(np.float64)


def striped8(idx):
    return np.asarray(idx).reshape(8, -1, 16).transpose(0, 2, 1).reshape(128, -1).astype(np.uint16)


def unstriped8(offs):
    return offs.reshape(8, 16, -1).transpose(0, 2, 1).reshape(8, -1).astype(np.int64)


def pick8(x, idx, run):
    r = np.arange(len(x))
    return x[r[:, None], idx[r % (8 * run) // run]]


E2M1 = np.array([0.0, 0.5, 1.0, 1.5, 2.0, 3.0, 4.0, 6.0, -0.0, -0.5, -1.0, -1.5, -2.0, -3.0, -4.0, -6.0])


def pack_weight(w, fmt):
    k, n = w.shape
    w = f64(np.asarray(w, np.float32).astype(ml_dtypes.bfloat16)).reshape(k // 32, 32, n)
    amax = np.abs(w).max(1)
    if fmt == "e4m3":
        byte = np.frexp(amax)[1] - 1 + 127 - 7
    else:
        mant, ex = np.frexp(amax / 6.0)
        byte = np.where(mant > 0.5, ex, ex - 1) + 127
    byte = np.clip(np.where(amax > 0, byte, 1), 1, 254)
    scaled = (w * np.exp2(127.0 - byte)[:, None, :]).reshape(k, n).astype(np.float32)
    by_word = np.ascontiguousarray(scaled.reshape(k // 512, 128, 4, n).transpose(0, 1, 3, 2))
    if fmt == "e4m3":
        words = by_word.astype(ml_dtypes.float8_e4m3fn).view(np.uint8)
    else:
        c = by_word.astype(ml_dtypes.float4_e2m1fn).view(np.uint8) & 0xF
        words = (c[..., 0::2] | (c[..., 1::2] << 4)).reshape(k // 512, 128, 2 * n)
    return np.ascontiguousarray(words), np.ascontiguousarray(byte.astype(np.uint8).reshape(k // 512, 16, n))


def unpack_weight(words, scales, fmt):
    g, _, n = scales.shape
    words = np.ascontiguousarray(words).reshape(g, 128, n, -1)
    if fmt == "e4m3":
        vals = words.view(ml_dtypes.float8_e4m3fn).astype(np.float64)
    else:
        nib = np.empty((g, 128, n, 4), np.uint8)
        nib[..., 0::2] = words & 0xF
        nib[..., 1::2] = words >> 4
        vals = E2M1[nib]
    vals = vals * np.repeat(np.exp2(scales.astype(np.float64) - 127.0), 8, axis=1)[..., None]
    return vals.transpose(0, 1, 3, 2).reshape(g * 512, n)


def softplus(v):
    return np.log(1.0 + np.exp(v))


D, T, I, Q = 512, 1024, 512, 128


def setup_inputs():
    n = np.random.standard_normal
    idx = np.stack([np.random.permutation(T)[:I] for _ in range(8)])
    idx2 = np.stack([np.random.permutation(T)[:I] for _ in range(8)])
    idx4 = np.stack([np.random.permutation(T)[:I] for _ in range(8)])
    fd = mx_kscale(D)
    keysp = pack_weight(n((D, T)) / fd[:, None], "e4m3")
    return {
        "query": (n((D, Q)) * 0.9 / np.sqrt(D) * fd[:, None]).astype(np.float32),
        "query2": (n((D, Q)) * 0.9 / np.sqrt(D) * fd[:, None]).astype(np.float32),
        "keys_words": keysp[0],
        "keys_scales": keysp[1],
        "lam": (np.random.uniform(0.6, 1.2, (Q, 1))).astype(np.float32),
        "lean": (np.random.uniform(0.2, 0.6, (Q, 1))).astype(np.float32),
        "old": (np.random.uniform(0.0, 2.0, (Q, T))).astype(np.float32),
        "gainm": (np.random.uniform(0.5, 1.5, (Q, I))).astype(np.float32),
        "offs": striped8(idx),
        "offs2": striped8(idx2),
        "offs4": striped8(idx4),
    }


def reference(query, query2, keys_words, keys_scales, lam, lean, old, gainm, offs, offs2, offs4):
    idx = unstriped8(offs)
    idx2 = unstriped8(offs2)
    idx4 = unstriped8(offs4)
    keysu = unpack_weight(keys_words, keys_scales, "e4m3")
    queryq = mxq(f64(query), 0, "e4m3")
    a = queryq.T @ keysu
    query2q = mxq(f64(query2), 0, "e4m3")
    b = query2q.T @ keysu
    s = pick8(a, idx, 16) / (softplus(pick8(b, idx2, 16)) + 0.5) * f64(lam)
    p = np.exp(s - np.max(s, axis=1, keepdims=True))
    r = p / np.sum(p, axis=1, keepdims=True)
    m0 = np.sum(r * s, axis=1, keepdims=True)
    dv0 = np.square(s - m0)
    v0 = np.sum(r * dv0, axis=1, keepdims=True)
    w = r * ((dv0 - v0) * f64(lean) + 1.0)
    ws = w * f64(gainm) * 256.0
    wf = np.zeros((Q, T))
    wf[np.arange(Q)[:, None], idx4[np.arange(Q) % 128 // 16]] = ws
    y = f64(old) + wf
    return y

@@ -1,0 +1,205 @@
+from contextlib import ExitStack
+
+import concourse.mybir as mybir
+
+D, T, SLOTS, Q = 512, 1024, 512, 128
+FLOPS = 2 * 2 * D * Q * T
+
+F32 = mybir.dt.float32
+BF16 = mybir.dt.bfloat16
+U32 = mybir.dt.uint32
+I32 = mybir.dt.int32
+U16 = mybir.dt.uint16
+U8 = mybir.dt.uint8
+FP8X4 = mybir.dt.float8_e4m3fn_x4
+ALU = mybir.AluOpType
+ACT = mybir.ActivationFunctionType
+
+P = 128
+PACK = 4
+BANK = 512
+HALF = SLOTS // 2
+NA = 160
+NB = SLOTS - NA
+EXP_CAP = 2.0**60
+OUT_PIECES = 4
+
+
+def tile_attend_worthfor_varyleaning_moved_heads_kernel(
+    tc, query, query2, keys_words, keys_scales, lam, lean, old, gainm, offs, offs2, offs4, out
+):
+    nc = tc.nc
+    with ExitStack() as ctx:
+        sb = ctx.enter_context(tc.tile_pool(name="sb", bufs=1))
+        psum = ctx.enter_context(tc.psum_pool(name="psum", bufs=1))
+
+        key_scales = sb.tile([P, T], U8, align_bytes=64, name="key_scales")
+        nc.vector.memset(key_scales[:].bitcast(I32), 0)
+        placed = sb.tile([P, T], F32, name="placed")
+        nc.vector.memset(placed[:], 0.0)
+
+        q2_raw = sb.tile([P, PACK, Q], F32, name="q2_raw")
+        nc.sync.dma_start(out=q2_raw[:], in_=query2.rearrange("(p j) q -> p j q", j=PACK))
+        words = keys_words[0].rearrange("p n t -> p (n t)")
+        key_words = [
+            sb.tile([P, BANK], U32, align_bytes=64, name="key_words%d" % h) for h in range(T // BANK)
+        ]
+        nc.sync.dma_start(out=key_words[0][:].bitcast(I32), in_=words[:, 0 : BANK * PACK].bitcast(I32))
+        for quad in range(4):
+            nc.sync.dma_start(
+                out=key_scales[32 * quad : 32 * quad + 4, :].bitcast(I32),
+                in_=keys_scales[0, 4 * quad : 4 * quad + 4, :].bitcast(I32),
+            )
+        nc.sync.dma_start(out=key_words[1][:].bitcast(I32), in_=words[:, BANK * PACK : T * PACK].bitcast(I32))
+        q_raw = sb.tile([P, PACK, Q], F32, name="q_raw")
+        nc.sync.dma_start(out=q_raw[:], in_=query.rearrange("(p j) q -> p j q", j=PACK))
+        list_b = sb.tile([P, SLOTS // 16], U16, name="list_b")
+        nc.sync.dma_start(list_b[:], offs2)
+        list_a = sb.tile([P, SLOTS // 16], U16, name="list_a")
+        nc.sync.dma_start(list_a[:], offs)
+        lam_col = sb.tile([P, 1], F32, name="lam_col")
+        nc.sync.dma_start(out=lam_col[:], in_=lam)
+        lean_col = sb.tile([P, 1], F32, name="lean_col")
+        nc.sync.dma_start(out=lean_col[:], in_=lean)
+        gain = sb.tile([P, SLOTS], F32, name="gain")
+        nc.sync.dma_start(out=gain[:], in_=gainm)
+        list_out = sb.tile([P, SLOTS // 16], U16, name="list_out")
+        nc.sync.dma_start(list_out[:], offs4)
+        old_sb = sb.tile([P, T], F32, name="old_sb")
+        nc.sync.dma_start(out=old_sb[:], in_=old)
+
+        def quantise(raw, name):
+            grouped = sb.tile([P, Q, PACK], BF16, align_bytes=64, name=name + "_grouped")
+            codes = sb.tile([P, Q], U32, align_bytes=64, name=name + "_codes")
+            scales = sb.tile([P, Q], U8, align_bytes=64, name=name + "_scales")
+            halves = (slice(0, Q // 2), slice(Q // 2, Q))
+            for cols in halves:
+                nc.vector.tensor_copy(out=grouped[:, cols, :], in_=raw[:, :, cols].rearrange("p j q -> p q j"))
+            for cols in halves:
+                nc.vector.quantize_mx(
+                    out=codes[:, cols].bitcast(FP8X4),
+                    scales=scales[:, cols],
+                    in_=grouped[:, cols, :].rearrange("p q j -> p (q j)"),
+                )
+            return codes, scales
+
+        def score(codes, scales, t0, n, name, bank):
+            acc = psum.tile([P, n], F32, name=name, tag="bank%d" % bank)
+            h, c0 = divmod(t0, BANK)
+            nc.tensor.matmul_mx(
+                out=acc[:],
+                lhsT=codes[:].bitcast(FP8X4),
+                lhsT_scale=scales[:],
+                rhs=key_words[h][:, c0 : c0 + n].bitcast(FP8X4),
+                rhs_scale=key_scales[:, t0 : t0 + n],
+                start=True,
+                stop=True,
+            )
+            return acc
+
+        q2_codes, q2_scales = quantise(q2_raw, "q2")
+        b_sb = sb.tile([P, T], F32, name="b_sb", tag="scores")
+        for i in range(4):
+            acc = score(q2_codes, q2_scales, i * 256, 256, "b_acc%d" % i, i)
+            if i < 3:
+                nc.scalar.copy(out=b_sb[:, i * 256 : (i + 1) * 256], in_=acc[:])
+            else:
+                nc.vector.tensor_copy(out=b_sb[:, i * 256 : (i + 1) * 256], in_=acc[:])
+
+        lo, hi = slice(0, HALF), slice(HALF, SLOTS)
+        lo16, hi16 = slice(0, HALF // 16), slice(HALF // 16, SLOTS // 16)
+        b_half = sb.tile([P, SLOTS], F32, name="b_half")
+        eb = sb.tile([P, SLOTS], F32, name="eb")
+        nc.vector.tensor_scalar(b_half[:, hi], b_sb[:].indirect(list_b[:, hi16]), 1.0, 0.5, ALU.mult, ALU.add)
+        nc.scalar.activation(eb[:, lo], b_sb[:].indirect(list_b[:, lo16]), ACT.Exp)
+        nc.scalar.activation(eb[:, hi], b_half[:, hi], ACT.Exp, bias=-0.5)
+        eb_cap = sb.tile([P, SLOTS], F32, name="eb_cap")
+        nc.gpsimd.tensor_scalar(eb_cap[:], eb[:], EXP_CAP, 0.0, ALU.min, ALU.max)
+        nc.vector.tensor_scalar(b_half[:, lo], b_sb[:].indirect(list_b[:, lo16]), 1.0, 0.5, ALU.mult, ALU.add)
+
+        q_codes, q_scales = quantise(q_raw, "q")
+        a_sb = sb.tile([P, T], F32, name="a_sb", tag="scores")
+        for h in range(T // BANK):
+            acc = score(q_codes, q_scales, h * BANK, BANK, "a_acc%d" % h, 4 + h)
+            nc.vector.tensor_copy(out=a_sb[:, h * BANK : (h + 1) * BANK], in_=acc[:])
+
+        neg_lam = sb.tile([P, 1], F32, name="neg_lam")
+        nc.gpsimd.tensor_scalar(neg_lam[:], lam_col[:], -1.0, 0.0, ALU.mult, ALU.add)
+        lean256 = sb.tile([P, 1], F32, name="lean256")
+        nc.gpsimd.tensor_scalar(lean256[:], lean_col[:], 256.0, 0.0, ALU.mult, ALU.add)
+
+        pa, pb = slice(0, NA), slice(NA, SLOTS)
+        shared = sb.tile([P, SLOTS + HALF], F32, name="shared")
+        picked_a = shared[:, 0:SLOTS]
+        soft = shared[:, HALF : SLOTS + HALF]
+        nc.vector.tensor_copy(picked_a[:, lo], a_sb[:].indirect(list_a[:, lo16]))
+        den = sb.tile([P, SLOTS], F32, name="den")
+        inv = sb.tile([P, SLOTS], F32, name="inv")
+        ln_den = sb.tile([P, SLOTS], F32, name="ln_den")
+        mid = NA + NB // 2
+        pieces = (slice(NA, mid), slice(mid, SLOTS))
+        for part in pieces + (pa,):
+            nc.scalar.activation(soft[:, part], eb_cap[:, part], ACT.Ln, bias=1.0)
+            nc.vector.scalar_tensor_tensor(den[:, part], soft[:, part], 0.5, b_half[:, part], ALU.add, ALU.max)
+        for part in pieces:
+            nc.scalar.activation(ln_den[:, part], den[:, part], ACT.Ln)
+        first = NA + 128
+        for part in (slice(NA, first), slice(first, SLOTS)):
+            nc.scalar.activation(inv[:, part], ln_den[:, part], ACT.Exp, scale=-1.0)
+        nc.vector.reciprocal(inv[:, pa], den[:, pa])
+        nc.vector.tensor_copy(picked_a[:, hi], a_sb[:].indirect(list_a[:, hi16]))
+
+        neg_s_min = sb.tile([P, SLOTS + 1], F32, name="neg_s_min")
+        neg_s = neg_s_min[:, 0:SLOTS]
+        neg_max = sb.tile([P, 1], F32, name="neg_max")
+        nc.vector.scalar_tensor_tensor(neg_s[:, pa], picked_a[:, pa], neg_lam[:], inv[:, pa], ALU.mult, ALU.mult)
+        nc.vector.tensor_reduce(neg_s_min[:, SLOTS : SLOTS + 1], neg_s[:, pa], mybir.AxisListType.X, ALU.min)
+        for part in (slice(NA, first), slice(first, SLOTS)):
+            nc.vector.scalar_tensor_tensor(
+                neg_s[:, part], picked_a[:, part], neg_lam[:], inv[:, part], ALU.mult, ALU.mult
+            )
+        nc.vector.tensor_reduce(neg_max[:], neg_s_min[:, NA : SLOTS + 1], mybir.AxisListType.X, ALU.min)
+
+        p = sb.tile([P, SLOTS], F32, name="p")
+        total = sb.tile([P, 1], F32, name="total")
+        nc.scalar.activation(p[:], neg_s, ACT.Exp, bias=neg_max[:], scale=-1.0, accum_out=total[:])
+        gap2 = sb.tile([P, SLOTS], F32, name="gap2")
+        nc.scalar.activation(gap2[:], neg_s, ACT.Square, bias=neg_max[:], scale=-1.0)
+        gap_p = sb.tile([P, SLOTS], F32, name="gap_p")
+        gap_sum = sb.tile([P, 1], F32, name="gap_sum")
+        nc.vector.scalar_tensor_tensor(
+            gap_p[:], neg_s, neg_max[:], p[:], ALU.subtract, ALU.mult, accum_out=gap_sum[:]
+        )
+        inv_total = sb.tile([P, 1], F32, name="inv_total")
+        nc.vector.reciprocal(inv_total[:], total[:])
+        gap2_p = sb.tile([P, SLOTS], F32, name="gap2_p")
+        gap2_sum = sb.tile([P, 1], F32, name="gap2_sum")
+        nc.vector.scalar_tensor_tensor(
+            gap2_p[:], gap2[:], lean256[:], p[:], ALU.mult, ALU.mult, accum_out=gap2_sum[:]
+        )
+        neg_mean = sb.tile([P, 1], F32, name="neg_mean")
+        nc.scalar.activation(neg_mean[:], gap_sum[:], ACT.Identity, bias=neg_max[:], scale=inv_total[:])
+        mean_gap2 = sb.tile([P, 1], F32, name="mean_gap2")
+        nc.scalar.activation(mean_gap2[:], gap_sum[:], ACT.Square, scale=inv_total[:])
+        dev2 = sb.tile([P, SLOTS], F32, name="dev2")
+        nc.scalar.activation(dev2[:], neg_s, ACT.Square, bias=neg_mean[:], scale=-1.0)
+        neg_inv_total = sb.tile([P, 1], F32, name="neg_inv_total")
+        nc.gpsimd.tensor_scalar(neg_inv_total[:], inv_total[:], -1.0, 0.0, ALU.mult, ALU.add)
+        base0 = sb.tile([P, 1], F32, name="base0")
+        nc.gpsimd.tensor_scalar(base0[:], mean_gap2[:], lean256[:], 256.0, ALU.mult, ALU.add)
+        base = sb.tile([P, 1], F32, name="base")
+        nc.scalar.activation(base[:], gap2_sum[:], ACT.Identity, bias=base0[:], scale=neg_inv_total[:])
+        tilt = sb.tile([P, SLOTS], F32, name="tilt")
+        share_gain = sb.tile([P, SLOTS], F32, name="share_gain")
+        nc.vector.scalar_tensor_tensor(share_gain[:], p[:], inv_total[:], gain[:], ALU.mult, ALU.mult)
+        nc.scalar.activation(tilt[:, 0:288], dev2[:, 0:288], ACT.Identity, bias=base[:], scale=lean256[:])
+        nc.vector.tensor_scalar(tilt[:, 288:], dev2[:, 288:], lean256[:], base[:], ALU.mult, ALU.add)
+        nc.vector.tensor_tensor(placed[:].indirect(list_out[:]), share_gain[:], tilt[:], ALU.mult)
+
+        edges = (0, 320, 640, 896, 1024)
+        for i in range(len(edges) - 1):
+            cols = slice(edges[i], edges[i + 1])
+            res = sb.tile([P, edges[i + 1] - edges[i]], F32, name="res%d" % i)
+            nc.vector.tensor_tensor(res[:], placed[:, cols], old_sb[:, cols], ALU.add)
+            queue = nc.sync if i % 2 == 0 else nc.scalar
+            queue.dma_start(out=out[:, cols], in_=res[:])

@@ -19,7 +19,7 @@ P = 128
 PACK = 4
 BANK = 512
 HALF = SLOTS // 2
-NA = 160
+NA = 144
 NB = SLOTS - NA
 EXP_CAP = 2.0**60
 OUT_PIECES = 4
@@ -57,10 +57,10 @@ def tile_attend_worthfor_varyleaning_moved_heads_kernel(
         nc.sync.dma_start(list_b[:], offs2)
         list_a = sb.tile([P, SLOTS // 16], U16, name="list_a")
         nc.sync.dma_start(list_a[:], offs)
-        lam_col = sb.tile([P, 1], F32, name="lam_col")
-        nc.sync.dma_start(out=lam_col[:], in_=lam)
         lean_col = sb.tile([P, 1], F32, name="lean_col")
-        nc.sync.dma_start(out=lean_col[:], in_=lean)
+        nc.gpsimd.dma_start(out=lean_col[:], in_=lean)
+        lam_col = sb.tile([P, 1], F32, name="lam_col")
+        nc.gpsimd.dma_start(out=lam_col[:], in_=lam)
         gain = sb.tile([P, SLOTS], F32, name="gain")
         nc.sync.dma_start(out=gain[:], in_=gainm)
         list_out = sb.tile([P, SLOTS // 16], U16, name="list_out")
@@ -101,10 +101,7 @@ def tile_attend_worthfor_varyleaning_moved_heads_kernel(
         b_sb = sb.tile([P, T], F32, name="b_sb", tag="scores")
         for i in range(4):
             acc = score(q2_codes, q2_scales, i * 256, 256, "b_acc%d" % i, i)
-            if i < 3:
-                nc.scalar.copy(out=b_sb[:, i * 256 : (i + 1) * 256], in_=acc[:])
-            else:
-                nc.vector.tensor_copy(out=b_sb[:, i * 256 : (i + 1) * 256], in_=acc[:])
+            nc.scalar.copy(out=b_sb[:, i * 256 : (i + 1) * 256], in_=acc[:])
 
         lo, hi = slice(0, HALF), slice(HALF, SLOTS)
         lo16, hi16 = slice(0, HALF // 16), slice(HALF // 16, SLOTS // 16)
@@ -123,10 +120,11 @@ def tile_attend_worthfor_varyleaning_moved_heads_kernel(
             acc = score(q_codes, q_scales, h * BANK, BANK, "a_acc%d" % h, 4 + h)
             nc.vector.tensor_copy(out=a_sb[:, h * BANK : (h + 1) * BANK], in_=acc[:])
 
-        neg_lam = sb.tile([P, 1], F32, name="neg_lam")
-        nc.gpsimd.tensor_scalar(neg_lam[:], lam_col[:], -1.0, 0.0, ALU.mult, ALU.add)
         lean256 = sb.tile([P, 1], F32, name="lean256")
         nc.gpsimd.tensor_scalar(lean256[:], lean_col[:], 256.0, 0.0, ALU.mult, ALU.add)
+
+        neg_lean256 = sb.tile([P, 1], F32, name="neg_lean256")
+        nc.gpsimd.tensor_scalar(neg_lean256[:], lean_col[:], -256.0, 0.0, ALU.mult, ALU.add)
 
         pa, pb = slice(0, NA), slice(NA, SLOTS)
         shared = sb.tile([P, SLOTS + HALF], F32, name="shared")
@@ -149,46 +147,46 @@ def tile_attend_worthfor_varyleaning_moved_heads_kernel(
         nc.vector.reciprocal(inv[:, pa], den[:, pa])
         nc.vector.tensor_copy(picked_a[:, hi], a_sb[:].indirect(list_a[:, hi16]))
 
-        neg_s_min = sb.tile([P, SLOTS + 1], F32, name="neg_s_min")
-        neg_s = neg_s_min[:, 0:SLOTS]
+        s_max = sb.tile([P, SLOTS + 1], F32, name="s_max")
+        s_val = s_max[:, 0:SLOTS]
         neg_max = sb.tile([P, 1], F32, name="neg_max")
-        nc.vector.scalar_tensor_tensor(neg_s[:, pa], picked_a[:, pa], neg_lam[:], inv[:, pa], ALU.mult, ALU.mult)
-        nc.vector.tensor_reduce(neg_s_min[:, SLOTS : SLOTS + 1], neg_s[:, pa], mybir.AxisListType.X, ALU.min)
+        nc.vector.scalar_tensor_tensor(s_val[:, pa], picked_a[:, pa], lam_col[:], inv[:, pa], ALU.mult, ALU.mult)
+        nc.vector.tensor_reduce(s_max[:, SLOTS : SLOTS + 1], s_val[:, pa], mybir.AxisListType.X, ALU.max)
         for part in (slice(NA, first), slice(first, SLOTS)):
             nc.vector.scalar_tensor_tensor(
-                neg_s[:, part], picked_a[:, part], neg_lam[:], inv[:, part], ALU.mult, ALU.mult
+                s_val[:, part], picked_a[:, part], lam_col[:], inv[:, part], ALU.mult, ALU.mult
             )
-        nc.vector.tensor_reduce(neg_max[:], neg_s_min[:, NA : SLOTS + 1], mybir.AxisListType.X, ALU.min)
+        nc.vector.tensor_reduce(neg_max[:], s_max[:, NA : SLOTS + 1], mybir.AxisListType.X, ALU.max, negate=True)
 
         p = sb.tile([P, SLOTS], F32, name="p")
         total = sb.tile([P, 1], F32, name="total")
-        nc.scalar.activation(p[:], neg_s, ACT.Exp, bias=neg_max[:], scale=-1.0, accum_out=total[:])
+        nc.scalar.activation(p[:], s_val, ACT.Exp, bias=neg_max[:], accum_out=total[:])
         gap2 = sb.tile([P, SLOTS], F32, name="gap2")
-        nc.scalar.activation(gap2[:], neg_s, ACT.Square, bias=neg_max[:], scale=-1.0)
+        nc.scalar.activation(gap2[:], s_val, ACT.Square, bias=neg_max[:])
+        row_max = sb.tile([P, 1], F32, name="row_max")
+        nc.scalar.activation(row_max[:], neg_max[:], ACT.Copy, scale=-1.0)
         gap_p = sb.tile([P, SLOTS], F32, name="gap_p")
         gap_sum = sb.tile([P, 1], F32, name="gap_sum")
         nc.vector.scalar_tensor_tensor(
-            gap_p[:], neg_s, neg_max[:], p[:], ALU.subtract, ALU.mult, accum_out=gap_sum[:]
+            gap_p[:], s_val, neg_max[:], p[:], ALU.add, ALU.mult, accum_out=gap_sum[:]
         )
         inv_total = sb.tile([P, 1], F32, name="inv_total")
         nc.vector.reciprocal(inv_total[:], total[:])
         gap2_p = sb.tile([P, SLOTS], F32, name="gap2_p")
         gap2_sum = sb.tile([P, 1], F32, name="gap2_sum")
         nc.vector.scalar_tensor_tensor(
-            gap2_p[:], gap2[:], lean256[:], p[:], ALU.mult, ALU.mult, accum_out=gap2_sum[:]
+            gap2_p[:], gap2[:], neg_lean256[:], p[:], ALU.mult, ALU.mult, accum_out=gap2_sum[:]
         )
-        neg_mean = sb.tile([P, 1], F32, name="neg_mean")
-        nc.scalar.activation(neg_mean[:], gap_sum[:], ACT.Identity, bias=neg_max[:], scale=inv_total[:])
+        mean = sb.tile([P, 1], F32, name="mean")
+        nc.scalar.activation(mean[:], gap_sum[:], ACT.Identity, bias=row_max[:], scale=inv_total[:])
         mean_gap2 = sb.tile([P, 1], F32, name="mean_gap2")
         nc.scalar.activation(mean_gap2[:], gap_sum[:], ACT.Square, scale=inv_total[:])
         dev2 = sb.tile([P, SLOTS], F32, name="dev2")
-        nc.scalar.activation(dev2[:], neg_s, ACT.Square, bias=neg_mean[:], scale=-1.0)
-        neg_inv_total = sb.tile([P, 1], F32, name="neg_inv_total")
-        nc.gpsimd.tensor_scalar(neg_inv_total[:], inv_total[:], -1.0, 0.0, ALU.mult, ALU.add)
+        nc.scalar.activation(dev2[:], s_val, ACT.Square, bias=mean[:], scale=-1.0)
         base0 = sb.tile([P, 1], F32, name="base0")
-        nc.gpsimd.tensor_scalar(base0[:], mean_gap2[:], lean256[:], 256.0, ALU.mult, ALU.add)
+        nc.scalar.activation(base0[:], mean_gap2[:], ACT.Identity, bias=256.0, scale=lean256[:])
         base = sb.tile([P, 1], F32, name="base")
-        nc.scalar.activation(base[:], gap2_sum[:], ACT.Identity, bias=base0[:], scale=neg_inv_total[:])
+        nc.scalar.activation(base[:], gap2_sum[:], ACT.Identity, bias=base0[:], scale=inv_total[:])
         tilt = sb.tile([P, SLOTS], F32, name="tilt")
         share_gain = sb.tile([P, SLOTS], F32, name="share_gain")
         nc.vector.scalar_tensor_tensor(share_gain[:], p[:], inv_total[:], gain[:], ALU.mult, ALU.mult)

from contextlib import ExitStack

import concourse.mybir as mybir

D, T, SLOTS, Q = 512, 1024, 512, 128
FLOPS = 2 * 2 * D * Q * T

F32 = mybir.dt.float32
BF16 = mybir.dt.bfloat16
U32 = mybir.dt.uint32
I32 = mybir.dt.int32
U16 = mybir.dt.uint16
U8 = mybir.dt.uint8
FP8X4 = mybir.dt.float8_e4m3fn_x4
ALU = mybir.AluOpType
ACT = mybir.ActivationFunctionType

P = 128
PACK = 4
BANK = 512
HALF = SLOTS // 2
NA = 144
NB = SLOTS - NA
EXP_CAP = 2.0**60
OUT_PIECES = 4


def tile_attend_worthfor_varyleaning_moved_heads_kernel(
    tc, query, query2, keys_words, keys_scales, lam, lean, old, gainm, offs, offs2, offs4, out
):
    nc = tc.nc
    with ExitStack() as ctx:
        sb = ctx.enter_context(tc.tile_pool(name="sb", bufs=1))
        psum = ctx.enter_context(tc.psum_pool(name="psum", bufs=1))

        key_scales = sb.tile([P, T], U8, align_bytes=64, name="key_scales")
        nc.vector.memset(key_scales[:].bitcast(I32), 0)
        placed = sb.tile([P, T], F32, name="placed")
        nc.vector.memset(placed[:], 0.0)

        q2_raw = sb.tile([P, PACK, Q], F32, name="q2_raw")
        nc.sync.dma_start(out=q2_raw[:], in_=query2.rearrange("(p j) q -> p j q", j=PACK))
        words = keys_words[0].rearrange("p n t -> p (n t)")
        key_words = [
            sb.tile([P, BANK], U32, align_bytes=64, name="key_words%d" % h) for h in range(T // BANK)
        ]
        nc.sync.dma_start(out=key_words[0][:].bitcast(I32), in_=words[:, 0 : BANK * PACK].bitcast(I32))
        for quad in range(4):
            nc.sync.dma_start(
                out=key_scales[32 * quad : 32 * quad + 4, :].bitcast(I32),
                in_=keys_scales[0, 4 * quad : 4 * quad + 4, :].bitcast(I32),
            )
        nc.sync.dma_start(out=key_words[1][:].bitcast(I32), in_=words[:, BANK * PACK : T * PACK].bitcast(I32))
        q_raw = sb.tile([P, PACK, Q], F32, name="q_raw")
        nc.sync.dma_start(out=q_raw[:], in_=query.rearrange("(p j) q -> p j q", j=PACK))
        list_b = sb.tile([P, SLOTS // 16], U16, name="list_b")
        nc.sync.dma_start(list_b[:], offs2)
        list_a = sb.tile([P, SLOTS // 16], U16, name="list_a")
        nc.sync.dma_start(list_a[:], offs)
        lean_col = sb.tile([P, 1], F32, name="lean_col")
        nc.gpsimd.dma_start(out=lean_col[:], in_=lean)
        lam_col = sb.tile([P, 1], F32, name="lam_col")
        nc.gpsimd.dma_start(out=lam_col[:], in_=lam)
        gain = sb.tile([P, SLOTS], F32, name="gain")
        nc.sync.dma_start(out=gain[:], in_=gainm)
        list_out = sb.tile([P, SLOTS // 16], U16, name="list_out")
        nc.sync.dma_start(list_out[:], offs4)
        old_sb = sb.tile([P, T], F32, name="old_sb")
        nc.sync.dma_start(out=old_sb[:], in_=old)

        def quantise(raw, name):
            grouped = sb.tile([P, Q, PACK], BF16, align_bytes=64, name=name + "_grouped")
            codes = sb.tile([P, Q], U32, align_bytes=64, name=name + "_codes")
            scales = sb.tile([P, Q], U8, align_bytes=64, name=name + "_scales")
            halves = (slice(0, Q // 2), slice(Q // 2, Q))
            for cols in halves:
                nc.vector.tensor_copy(out=grouped[:, cols, :], in_=raw[:, :, cols].rearrange("p j q -> p q j"))
            for cols in halves:
                nc.vector.quantize_mx(
                    out=codes[:, cols].bitcast(FP8X4),
                    scales=scales[:, cols],
                    in_=grouped[:, cols, :].rearrange("p q j -> p (q j)"),
                )
            return codes, scales

        def score(codes, scales, t0, n, name, bank):
            acc = psum.tile([P, n], F32, name=name, tag="bank%d" % bank)
            h, c0 = divmod(t0, BANK)
            nc.tensor.matmul_mx(
                out=acc[:],
                lhsT=codes[:].bitcast(FP8X4),
                lhsT_scale=scales[:],
                rhs=key_words[h][:, c0 : c0 + n].bitcast(FP8X4),
                rhs_scale=key_scales[:, t0 : t0 + n],
                start=True,
                stop=True,
            )
            return acc

        q2_codes, q2_scales = quantise(q2_raw, "q2")
        b_sb = sb.tile([P, T], F32, name="b_sb", tag="scores")
        for i in range(4):
            acc = score(q2_codes, q2_scales, i * 256, 256, "b_acc%d" % i, i)
            nc.scalar.copy(out=b_sb[:, i * 256 : (i + 1) * 256], in_=acc[:])

        lo, hi = slice(0, HALF), slice(HALF, SLOTS)
        lo16, hi16 = slice(0, HALF // 16), slice(HALF // 16, SLOTS // 16)
        b_half = sb.tile([P, SLOTS], F32, name="b_half")
        eb = sb.tile([P, SLOTS], F32, name="eb")
        nc.vector.tensor_scalar(b_half[:, hi], b_sb[:].indirect(list_b[:, hi16]), 1.0, 0.5, ALU.mult, ALU.add)
        nc.scalar.activation(eb[:, lo], b_sb[:].indirect(list_b[:, lo16]), ACT.Exp)
        nc.scalar.activation(eb[:, hi], b_half[:, hi], ACT.Exp, bias=-0.5)
        eb_cap = sb.tile([P, SLOTS], F32, name="eb_cap")
        nc.gpsimd.tensor_scalar(eb_cap[:], eb[:], EXP_CAP, 0.0, ALU.min, ALU.max)
        nc.vector.tensor_scalar(b_half[:, lo], b_sb[:].indirect(list_b[:, lo16]), 1.0, 0.5, ALU.mult, ALU.add)

        q_codes, q_scales = quantise(q_raw, "q")
        a_sb = sb.tile([P, T], F32, name="a_sb", tag="scores")
        for h in range(T // BANK):
            acc = score(q_codes, q_scales, h * BANK, BANK, "a_acc%d" % h, 4 + h)
            nc.vector.tensor_copy(out=a_sb[:, h * BANK : (h + 1) * BANK], in_=acc[:])

        lean256 = sb.tile([P, 1], F32, name="lean256")
        nc.gpsimd.tensor_scalar(lean256[:], lean_col[:], 256.0, 0.0, ALU.mult, ALU.add)

        neg_lean256 = sb.tile([P, 1], F32, name="neg_lean256")
        nc.gpsimd.tensor_scalar(neg_lean256[:], lean_col[:], -256.0, 0.0, ALU.mult, ALU.add)

        pa, pb = slice(0, NA), slice(NA, SLOTS)
        shared = sb.tile([P, SLOTS + HALF], F32, name="shared")
        picked_a = shared[:, 0:SLOTS]
        soft = shared[:, HALF : SLOTS + HALF]
        nc.vector.tensor_copy(picked_a[:, lo], a_sb[:].indirect(list_a[:, lo16]))
        den = sb.tile([P, SLOTS], F32, name="den")
        inv = sb.tile([P, SLOTS], F32, name="inv")
        ln_den = sb.tile([P, SLOTS], F32, name="ln_den")
        mid = NA + NB // 2
        pieces = (slice(NA, mid), slice(mid, SLOTS))
        for part in pieces + (pa,):
            nc.scalar.activation(soft[:, part], eb_cap[:, part], ACT.Ln, bias=1.0)
            nc.vector.scalar_tensor_tensor(den[:, part], soft[:, part], 0.5, b_half[:, part], ALU.add, ALU.max)
        for part in pieces:
            nc.scalar.activation(ln_den[:, part], den[:, part], ACT.Ln)
        first = NA + 128
        for part in (slice(NA, first), slice(first, SLOTS)):
            nc.scalar.activation(inv[:, part], ln_den[:, part], ACT.Exp, scale=-1.0)
        nc.vector.reciprocal(inv[:, pa], den[:, pa])
        nc.vector.tensor_copy(picked_a[:, hi], a_sb[:].indirect(list_a[:, hi16]))

        s_max = sb.tile([P, SLOTS + 1], F32, name="s_max")
        s_val = s_max[:, 0:SLOTS]
        neg_max = sb.tile([P, 1], F32, name="neg_max")
        nc.vector.scalar_tensor_tensor(s_val[:, pa], picked_a[:, pa], lam_col[:], inv[:, pa], ALU.mult, ALU.mult)
        nc.vector.tensor_reduce(s_max[:, SLOTS : SLOTS + 1], s_val[:, pa], mybir.AxisListType.X, ALU.max)
        for part in (slice(NA, first), slice(first, SLOTS)):
            nc.vector.scalar_tensor_tensor(
                s_val[:, part], picked_a[:, part], lam_col[:], inv[:, part], ALU.mult, ALU.mult
            )
        nc.vector.tensor_reduce(neg_max[:], s_max[:, NA : SLOTS + 1], mybir.AxisListType.X, ALU.max, negate=True)

        p = sb.tile([P, SLOTS], F32, name="p")
        total = sb.tile([P, 1], F32, name="total")
        nc.scalar.activation(p[:], s_val, ACT.Exp, bias=neg_max[:], accum_out=total[:])
        gap2 = sb.tile([P, SLOTS], F32, name="gap2")
        nc.scalar.activation(gap2[:], s_val, ACT.Square, bias=neg_max[:])
        row_max = sb.tile([P, 1], F32, name="row_max")
        nc.scalar.activation(row_max[:], neg_max[:], ACT.Copy, scale=-1.0)
        gap_p = sb.tile([P, SLOTS], F32, name="gap_p")
        gap_sum = sb.tile([P, 1], F32, name="gap_sum")
        nc.vector.scalar_tensor_tensor(
            gap_p[:], s_val, neg_max[:], p[:], ALU.add, ALU.mult, accum_out=gap_sum[:]
        )
        inv_total = sb.tile([P, 1], F32, name="inv_total")
        nc.vector.reciprocal(inv_total[:], total[:])
        gap2_p = sb.tile([P, SLOTS], F32, name="gap2_p")
        gap2_sum = sb.tile([P, 1], F32, name="gap2_sum")
        nc.vector.scalar_tensor_tensor(
            gap2_p[:], gap2[:], neg_lean256[:], p[:], ALU.mult, ALU.mult, accum_out=gap2_sum[:]
        )
        mean = sb.tile([P, 1], F32, name="mean")
        nc.scalar.activation(mean[:], gap_sum[:], ACT.Identity, bias=row_max[:], scale=inv_total[:])
        mean_gap2 = sb.tile([P, 1], F32, name="mean_gap2")
        nc.scalar.activation(mean_gap2[:], gap_sum[:], ACT.Square, scale=inv_total[:])
        dev2 = sb.tile([P, SLOTS], F32, name="dev2")
        nc.scalar.activation(dev2[:], s_val, ACT.Square, bias=mean[:], scale=-1.0)
        base0 = sb.tile([P, 1], F32, name="base0")
        nc.scalar.activation(base0[:], mean_gap2[:], ACT.Identity, bias=256.0, scale=lean256[:])
        base = sb.tile([P, 1], F32, name="base")
        nc.scalar.activation(base[:], gap2_sum[:], ACT.Identity, bias=base0[:], scale=inv_total[:])
        tilt = sb.tile([P, SLOTS], F32, name="tilt")
        share_gain = sb.tile([P, SLOTS], F32, name="share_gain")
        nc.vector.scalar_tensor_tensor(share_gain[:], p[:], inv_total[:], gain[:], ALU.mult, ALU.mult)
        nc.scalar.activation(tilt[:, 0:288], dev2[:, 0:288], ACT.Identity, bias=base[:], scale=lean256[:])
        nc.vector.tensor_scalar(tilt[:, 288:], dev2[:, 288:], lean256[:], base[:], ALU.mult, ALU.add)
        nc.vector.tensor_tensor(placed[:].indirect(list_out[:]), share_gain[:], tilt[:], ALU.mult)

        edges = (0, 320, 640, 896, 1024)
        for i in range(len(edges) - 1):
            cols = slice(edges[i], edges[i + 1])
            res = sb.tile([P, edges[i + 1] - edges[i]], F32, name="res%d" % i)
            nc.vector.tensor_tensor(res[:], placed[:, cols], old_sb[:, cols], ALU.add)
            queue = nc.sync if i % 2 == 0 else nc.scalar
            queue.dma_start(out=out[:, cols], in_=res[:])
